import numpy as np, ml_dtypes
CORES = [8,136,40,168]
N = 4
import mx_ref
NC, G, MB = 128, 4, 2
C = np.float32(0.029)
BF = ml_dtypes.bfloat16
def cut(t, i, w=512):
    return t[:, w * i:w * i + w]
def tile(rs):
    return np.stack(rs, axis=2).reshape(128, -1).astype(BF)
def layer(w, X):
    out = []
    for i in range(G):
        for t in range(len(X)):
            p = mx_ref.matmul(mx_ref.quantize(cut(w, len(X) * i + t)), X[t])
            z = p if t == 0 else z + p
        out.append(z)
    return out
def act(Z):
    return [np.maximum(z, 0) * C for z in Z]
def masked(U, Z):
    return [(u * (z > 0)) * C for u, z in zip(U, Z)]
def setup_inputs(rng):
    def f(*shape):
        return mx_ref.flush((rng.standard_normal(shape, dtype=np.float32) * np.exp2(rng.integers(-2, 3, shape[:-1] + (1,)))).astype(BF))
    return {"x": f(N, 128, MB * 4 * NC), "e": f(N, 128, MB * 4 * NC), "w": f(N, 128, G * 512), "v": f(N, 128, G * 512)}
def setup_inputs_blocks(rng):
    d = setup_inputs(rng)
    for k in ("x", "e"): d[k] = mx_ref.spread(d[k], rng, 4)
    for k in ("w", "v"): d[k] = mx_ref.spread(d[k], rng, 1)
    return d
def setup_inputs_wide(rng):
    d = setup_inputs(rng)
    for k in ("x", "e"): d[k] = mx_ref.flush((d[k].astype(np.float32) * np.exp2(rng.integers(-8, 9, (N, 1, 1))).astype(np.float32)).astype(BF))
    return d
def setup_inputs_zeros(rng):
    d = setup_inputs(rng); v = d["x"].reshape(N, 128, -1, 4).copy()
    v[np.broadcast_to((rng.random((N, 1, v.shape[2], 1)) < 0.33), v.shape)] = 0
    d["x"] = v.reshape(d["x"].shape)
    return d
def reference(x, e, w, v):
    y = np.full((N, 128, MB * G * NC), np.nan, np.float32)
    for m in range(MB):
        a = mx_ref.quantize(cut(x[N - 1], m, 4 * NC)); Z = []
        for s in range(N):
            Z.append(layer(w[s], [a]))
            if s < N - 1: a = mx_ref.quantize(tile(act(Z[s])))
        b = mx_ref.quantize(cut(e[0], m, 4 * NC))
        for s in range(N - 1, 0, -1):
            b = mx_ref.quantize(tile(masked(layer(v[s], [b]), Z[s])))
        U = layer(v[0], [b])
        for i in range(G):
            y[0][:, NC * (G * m + i):NC * (G * m + i) + NC] = U[i] * (Z[0][i] > 0)
    return {"y": y}

from concourse.bass import DstId, RemoteDMATransfer
from concourse.mybir import dt, AluOpType, ActivationFunctionType

M, G, NC = 2, 4, 128
C = 0.029

SCRATCH = {
    "wb": ("sbuf", [128, G * 512], "bfloat16"),
    "vb": ("sbuf", [128, G * 512], "bfloat16"),
    "xb": ("sbuf", [128, M * 512], "bfloat16"),
    "eb": ("sbuf", [128, M * 512], "bfloat16"),
    "wq": ("sbuf", [128, G * NC], "float8_e4m3fn_x4"), "ws": ("sbuf", [128, G * NC], "uint8"),
    "vq": ("sbuf", [128, G * NC], "float8_e4m3fn_x4"), "vs": ("sbuf", [128, G * NC], "uint8"),
    "rq": ("sbuf", [128, NC], "float8_e4m3fn_x4"), "rs": ("sbuf", [128, NC], "uint8"),
    "yb": ("sbuf", [128, M * G * NC], "float32"),
}
SEMAPHORES = ["arr_r", "la", "lb", "lr", "yst", "y0", "y1a", "y1b"]
for _m in range(M):
    for _k in "aobp":
        SCRATCH["%sq%d" % (_k, _m)] = ("sbuf", [128, NC], "float8_e4m3fn_x4")
        SCRATCH["%ss%d" % (_k, _m)] = ("sbuf", [128, NC], "uint8")
    SCRATCH["hd%d" % _m] = ("sbuf", [128, 512], "bfloat16")
    SCRATCH["hb%d" % _m] = ("sbuf", [128, 512], "bfloat16")
    SCRATCH["mk%d" % _m] = ("sbuf", [128, G * NC], "float32")
    SCRATCH["z%d" % _m] = ("psum", [128, 512 * G], "float32")
    SEMAPHORES += ["%s%d" % (_k, _m) for _k in ("lx", "lw", "lv", "qw", "qv", "arr_a", "arr_b", "hd", "hb", "od", "pd", "mk")]
    SEMAPHORES += ["%s%d_%d" % (_k, _m, _i) for _k in ("zd", "ud", "mi") for _i in range(G)]


def rank_program(g, core, T, topo):
    rank = T.rank_of(core)
    if rank is None:
        return
    last = len(T.cores) - 1
    sem = T.sem
    P, V, S, Y = g.tensor, g.vector, g.scalar, g.sync

    def bank(z, i):
        return T["z%d" % z][:, 512 * i:512 * i + NC]

    def mask(m, i):
        return T["mk%d" % m][:, NC * i:NC * i + NC]

    def load(q, name, buf, s, h, cols):
        q.dma_start(T[buf][:, cols * h:cols * h + cols], T[name][:, cols * h:cols * h + cols]).then_inc(sem["%s%d" % (s, h)], 16)

    def quantise_weights(k):
        for h in range(2):
            V.wait_ge(sem["l%s%d" % (k, h)], 16)
            V.quantize_mx(T[k + "q"][:, 256 * h:256 * h + 256], T[k + "s"][:, 256 * h:256 * h + 256],
                          T[k + "b"][:, 1024 * h:1024 * h + 1024]).then_inc(sem["q%s%d" % (k, h)], 1)

    def quantise_input(buf, out, done):
        for m in range(M):
            V.wait_ge(sem["lx%d" % m], 16)
            V.quantize_mx(T["%sq%d" % (out, m)][:], T["%ss%d" % (out, m)][:], T[buf][:, 512 * m:512 * m + 512]).then_inc(sem["%s%d" % (done, m)], 1)

    def products(k, side, m, z, done):
        for i in range(G):
            if m == 0 and i % 2 == 0:
                P.wait_ge(sem["q%s%d" % (k, i // 2)], 1)
            P.matmul_mx(bank(z, i), T[k + "q"][:, NC * i:NC * i + NC], T[k + "s"][:, NC * i:NC * i + NC],
                        T["%sq%d" % (side, m)][:], T["%ss%d" % (side, m)][:], True, True).then_inc(sem["%s%d_%d" % (done, m, i)], 1)

    def send(dst, sq, ss, dq, ds, arr, loc):
        rid, pid = topo.addr(dst, core)
        eng = topo.mask(core, dst)
        g.remote_dma(T[dq][:].bitcast(dt.uint8), T[sq][:].bitcast(dt.uint8), sem[arr], sem[loc], pid, rid, eng)
        g.remote_dma(T[ds][:], T[ss][:], sem[arr], sem[loc], pid, rid, eng)
        return 2 * bin(eng).count("1")

    def send_tile(dst, out, into, m, done, loc):
        g.wait_ge(sem["%s%d" % (done, m)], 1)
        return send(dst, "%sq%d" % (out, m), "%ss%d" % (out, m), "%sq%d" % (into, m), "%ss%d" % (into, m), "arr_%s%d" % (into, m), loc)

    def inc_of(src, dst):
        return 2 * bin(topo.mask(src, dst)).count("1")

    def halves(eng):
        bits = [1 << k for k in range(16) if eng >> k & 1]
        n = len(bits) // 2
        return sum(bits[:n]), sum(bits[n:])

    down_from = T.cores[rank - 1 if rank > 0 else last]
    down_to = T.cores[rank + 1 if rank < last else 0]
    via = [T.cores[1 + m] for m in range(M)]
    left_a = M * inc_of(core, down_to)

    if rank == 0:
        load(Y, "e", "eb", "lx", 0, 512)
        load(S, "e", "eb", "lx", 1, 512)
        load(Y, "w", "wb", "lw", 0, 1024)
        load(S, "w", "wb", "lw", 1, 1024)
        Y.wait_ge(sem.la, left_a)
        load(Y, "v", "vb", "lv", 0, 1024)
        load(Y, "v", "vb", "lv", 1, 1024)
    elif rank == last:
        load(Y, "x", "xb", "lx", 0, 512)
        load(Y, "x", "xb", "lx", 1, 512)
        for h, q in enumerate((Y, S)):
            q.wait_ge(sem.la, left_a)
            load(q, "v", "vb", "lv", h, 1024)
            load(q, "w", "wb", "lw", h, 1024)
    else:
        for h, q in enumerate((Y, S)):
            load(q, "w", "wb", "lw", h, 1024)
            load(q, "v", "vb", "lv", h, 1024)

    if rank == 0:
        quantise_input("eb", "p", "pd")
    if rank == last:
        quantise_input("xb", "o", "od")
        quantise_weights("v")
    quantise_weights("w")
    if 0 < rank < last:
        quantise_weights("v")

    left_b = left_r = 0
    if rank == 0:
        for m in range(M):
            g.wait_ge(sem["pd%d" % m], 1)
        engs = halves(topo.mask(core, via[0]) & topo.mask(core, via[1]))
        dst = []
        for c in via:
            rid, pid = topo.addr(c, core)
            dst.append(DstId(rid=rid, pnc=pid))
        for part in "qs":
            tr = []
            for m in range(M):
                a, b = T["p%s%d" % (part, m)][:], T["r%s" % part][:]
                if part == "q":
                    a, b = a.bitcast(dt.uint8), b.bitcast(dt.uint8)
                tr.append(RemoteDMATransfer(dst_ids=[dst[m]], dma_engine_mask=engs[m], remote_sem=sem.arr_r, src=a, dst=b))
                left_b += bin(engs[m]).count("1")
            g.remote_dma_fused(tr, local_sem=sem.lb)
    elif core in via:
        m = via.index(core)
        g.wait_ge(sem.arr_r, 2 * bin(halves(topo.mask(T.cores[0], via[0]) & topo.mask(T.cores[0], via[1]))[m]).count("1"))
        left_r += send(T.cores[last], "rq", "rs", "bq%d" % m, "bs%d" % m, "arr_b%d" % m, "lr")
    for m in range(M):
        send_tile(down_to, "o", "a", m, "od", "la")
    if rank > 0:
        for m in range(M):
            left_b += send_tile(T.cores[rank - 1], "p", "b", m, "pd", "lb")
    g.wait_ge(sem.la, left_a)
    g.wait_ge(sem.lb, left_b)
    if left_r:
        g.wait_ge(sem.lr, left_r)

    def await_down(m):
        P.wait_ge(sem["arr_a%d" % m], inc_of(down_from, core))

    def await_back(m):
        P.wait_ge(sem["arr_b%d" % m], inc_of(via[m] if rank == last else T.cores[rank + 1], core))

    if rank == last:
        for m in range(M):
            if m > 0:
                P.wait_ge(sem["hb%d" % (m - 1)], G)
            await_back(m)
            products("v", "b", m, 1, "ud")
            await_down(m)
            products("w", "a", m, 0, "zd")

            def make_mask(i):
                V.wait_ge(sem["zd%d_%d" % (m, i)], 1)
                V.tensor_scalar(mask(m, i), bank(0, i), 0.0, C, AluOpType.is_gt, AluOpType.mult).then_inc(sem["mi%d_%d" % (m, i)], 1)

            def use_mask(i):
                V.wait_ge(sem["ud%d_%d" % (m, i)], 1)
                V.wait_ge(sem["mi%d_%d" % (m, i)], 1)
                V.tensor_tensor(T["hb%d" % m][:, i:4 * NC:4], bank(1, i), mask(m, i), AluOpType.mult).then_inc(sem["hb%d" % m], 1)

            for i in range(G + 1):
                if i < G:
                    make_mask(i)
                if i > 0:
                    use_mask(i - 1)
            V.wait_ge(sem["hb%d" % m], G)
            V.quantize_mx(T["pq%d" % m][:], T["ps%d" % m][:], T["hb%d" % m][:]).then_inc(sem["pd%d" % m], 1)
        return

    for m in range(M):
        await_down(m)
        products("w", "a", m, m, "zd")
        for i in range(G):
            out = T["hd%d" % m][:, i:4 * NC:4]
            if i % 2 == 0:
                S.wait_ge(sem["zd%d_%d" % (m, i)], 1)
                S.activation(out, bank(m, i), ActivationFunctionType.Relu, scale=C).then_inc(sem["hd%d" % m], 1)
            else:
                V.wait_ge(sem["zd%d_%d" % (m, i)], 1)
                V.tensor_scalar(out, bank(m, i), 0.0, C, AluOpType.max, AluOpType.mult).then_inc(sem["hd%d" % m], 1)
        V.wait_ge(sem["hd%d" % m], G)
        V.quantize_mx(T["oq%d" % m][:], T["os%d" % m][:], T["hd%d" % m][:]).then_inc(sem["od%d" % m], 1)
    for m in range(M):
        for i in range(G):
            V.wait_ge(sem["zd%d_%d" % (m, i)], 1)
            if rank == 0:
                V.tensor_scalar(mask(m, i), bank(m, i), 0.0, None, AluOpType.is_gt).then_inc(sem["mk%d" % m], 1)
            else:
                V.tensor_scalar(mask(m, i), bank(m, i), 0.0, C, AluOpType.is_gt, AluOpType.mult).then_inc(sem["mk%d" % m], 1)
    if rank == 0:
        quantise_weights("v")

    for m in range(M):
        P.wait_ge(sem["mk%d" % m], G)
        await_back(m)
        products("v", "b", m, m, "ud")
        V.wait_ge(sem["mk%d" % m], G)
        for i in range(G):
            V.wait_ge(sem["ud%d_%d" % (m, i)], 1)
            if rank > 0:
                V.tensor_tensor(T["hb%d" % m][:, i:4 * NC:4], bank(m, i), mask(m, i), AluOpType.mult).then_inc(sem["hb%d" % m], 1)
            else:
                done = sem.y0 if m == 0 else (sem.y1a if i < 2 else sem.y1b)
                k = NC * (G * m + i)
                V.tensor_tensor(T.yb[:, k:k + NC], bank(m, i), mask(m, i), AluOpType.mult).then_inc(done, 1)
        if rank > 0:
            V.wait_ge(sem["hb%d" % m], G)
            V.quantize_mx(T["pq%d" % m][:], T["ps%d" % m][:], T["hb%d" % m][:]).then_inc(sem["pd%d" % m], 1)
    if rank == 0:
        n = G * NC
        Y.wait_ge(sem.y0, G)
        Y.dma_start(T.y[:, 0:n], T.yb[:, 0:n]).then_inc(sem.yst, 16)
        Y.wait_ge(sem.y1a, 2)
        Y.dma_start(T.y[:, n:n + 256], T.yb[:, n:n + 256]).then_inc(sem.yst, 16)
        S.wait_ge(sem.y1b, 2)
        S.dma_start(T.y[:, n + 256:n + 512], T.yb[:, n + 256:n + 512]).then_inc(sem.yst, 16)
        Y.wait_ge(sem.yst, 48)
